import numpy as np
import ml_dtypes


def mxq(x, axis, fmt="e4m3"):
    dtype, down = {"e4m3": (ml_dtypes.float8_e4m3fn, 7), "e5m2": (ml_dtypes.float8_e5m2, 14)}[fmt]
    v = np.moveaxis(np.asarray(x, np.float32).astype(ml_dtypes.bfloat16).astype(np.float64), axis, -1)
    blocks = v.reshape(v.shape[:-1] + (-1, 32))
    amax = np.abs(blocks).max(-1, keepdims=True)
    byte = np.maximum(np.where(amax > 0, np.frexp(amax)[1] - 1 + 127, 0) - down, 1)
    scale = np.exp2(byte - 127.0)
    codes = (blocks / scale).astype(np.float32).astype(dtype).astype(np.float64)
    return np.moveaxis((codes * scale).reshape(v.shape), -1, axis)


WIDE = False


def mx_kscale(k):
    if not WIDE:
        return np.ones(k)
    levels = np.array([10, -10, 5, -5, 0])
    if k % 512:
        return np.exp2(np.random.permutation(np.resize(levels, k // 32))).repeat(32)
    a = np.empty((k // 512, 16))
    for p in range(k // 512):
        a[p, :8] = np.random.permutation(np.resize(levels, 8))
        for g in range(8):
            far = levels[np.abs(levels - a[p, g]) >= 10]
            a[p, g + 8] = far[np.random.randint(len(far))]
    return np.exp2(a.ravel()).repeat(32)


def f64(x):
    return np.asarray(x).astype(np.float64)


def striped(idx):
    return np.tile(np.asarray(idx).reshape(-1, 16).T, (8, 1)).astype(np.uint16)


def unstriped(offs):
    return offs[:16].T.reshape(-1).astype(np.int64)


D, T, I, Q = 512, 1024, 256, 512


def setup_inputs():
    n = np.random.standard_normal
    idx = np.random.permutation(T)[:I]
    idx2 = np.random.permutation(T)[:I]
    fd = mx_kscale(D)
    fq = mx_kscale(Q)
    return {
        "query": (n((D, Q)) * 0.6 / np.sqrt(D) * fd[:, None]).astype(np.float32),
        "keys": (n((D, T)) / fd[:, None]).astype(np.float32),
        "mass": np.tile(np.random.uniform(0.5, 4.0, T), (128, 1)).astype(np.float32),
        "target": (np.random.uniform(0.0, 0.008, (Q, I))).astype(np.float32),
        "qs": (np.random.uniform(16.0, 64.0, (Q, 1)) * fq[:, None]).astype(np.float32),
        "qrows": (n((Q, D)) / fq[:, None]).astype(np.float32),
        "old": (n((D, T)) * 1.0).astype(np.float32),
        "offs": striped(idx),
        "offs2": striped(idx2),
    }


def reference(query, keys, mass, target, qs, qrows, old, offs, offs2):
    idx = unstriped(offs)
    idx2 = unstriped(offs2)
    km = (f64(keys)[:, idx] * f64(mass)[:1][:, idx] + f64(keys)[:, idx2] * f64(mass)[:1][:, idx2]) / (f64(mass)[:1][:, idx] + f64(mass)[:1][:, idx2])
    queryq = mxq(f64(query), 0, "e4m3")
    kmq = mxq(km, 0, "e4m3")
    a = queryq.T @ kmq
    s = a + np.log(f64(mass)[:1][:, idx] + f64(mass)[:1][:, idx2])
    p = np.exp(s - np.max(s, axis=1, keepdims=True))
    ds = (p / np.sum(p, axis=1, keepdims=True) - f64(target)) * f64(qs)
    qrowsq = mxq(f64(qrows), 0, "e4m3")
    dsq = mxq(ds, 0, "e4m3")
    gk = qrowsq.T @ dsq
    g1 = gk * f64(mass)[:1][:, idx] / (f64(mass)[:1][:, idx] + f64(mass)[:1][:, idx2])
    g2 = gk * f64(mass)[:1][:, idx2] / (f64(mass)[:1][:, idx] + f64(mass)[:1][:, idx2])
    fa = np.zeros((D, T))
    fa[:, idx] = g1
    fb = np.zeros((D, T))
    fb[:, idx2] = g2
    y = f64(old) + fa + fb
    return y

@@ -1,0 +1,276 @@
+from contextlib import ExitStack
+
+import concourse.mybir as mybir
+from concourse.masks import make_identity
+
+D, T, I, Q = 512, 1024, 256, 512
+FLOPS = 2 * D * Q * I * 2
+
+F32 = mybir.dt.float32
+BF16 = mybir.dt.bfloat16
+U32 = mybir.dt.uint32
+U16 = mybir.dt.uint16
+U8 = mybir.dt.uint8
+FP8X4 = mybir.dt.float8_e4m3fn_x4
+ALU = mybir.AluOpType
+ACT = mybir.ActivationFunctionType
+AX = mybir.AxisListType
+
+P = 128
+PACK = 4
+HALF = I // 2
+EARLY = 2
+BANK = 512
+
+
+def tile_attend_bmassmerge_kernel(tc, query, keys, mass, target, qs, qrows, old, offs, offs2, out):
+    nc = tc.nc
+    with ExitStack() as ctx:
+        held = ctx.enter_context(tc.tile_pool(name="held", bufs=1))
+        ring = ctx.enter_context(tc.tile_pool(name="ring", bufs=3))
+        ps_small = ctx.enter_context(tc.psum_pool(name="ps_small", bufs=2))
+        ps_sum = ctx.enter_context(tc.psum_pool(name="ps_sum", bufs=6))
+
+        list1 = held.tile([P, I // 16], U16, name="list1")
+        list2 = held.tile([P, I // 16], U16, name="list2")
+        lists = (list1, list2)
+        mass_sb = held.tile([P, T], F32, name="mass_sb")
+        key_planes = [held.tile([P, T], F32, name=f"key_plane{t}") for t in range(PACK)]
+        query_sb = [held.tile([P, PACK, Q // 2], F32, name=f"query_sb{h}") for h in range(2)]
+        qrows_sb = [held.tile([P, PACK, D // 2], F32, name=f"qrows_sb{h}") for h in range(2)]
+        target_sb = held.tile([P, PACK, I], F32, name="target_sb")
+        qs_sb = held.tile([P, PACK], F32, name="qs_sb")
+        old_sb = [held.tile([P, T], F32, name=f"old_sb{j}") for j in range(PACK)]
+
+        keys_v = keys.rearrange("(p t) n -> p t n", t=PACK)
+        query_v = query.rearrange("(p j) q -> p j q", j=PACK)
+        qrows_v = qrows.rearrange("(p j) d -> p j d", j=PACK)
+        nc.sync.dma_start(mass_sb[:], mass)
+        nc.sync.dma_start(list1[:], offs)
+        nc.sync.dma_start(list2[:], offs2)
+        nc.sync.dma_start(key_planes[0][:], keys_v[:, 0, :])
+        nc.sync.dma_start(key_planes[1][:], keys_v[:, 1, :])
+        nc.sync.dma_start(query_sb[0][:], query_v[:, :, 0 : Q // 2])
+        nc.sync.dma_start(key_planes[2][:], keys_v[:, 2, :])
+        nc.sync.dma_start(key_planes[3][:], keys_v[:, 3, :])
+        nc.sync.dma_start(query_sb[1][:], query_v[:, :, Q // 2 : Q])
+        nc.sync.dma_start(qs_sb[:], qs.rearrange("(p r) o -> p (r o)", r=PACK))
+        nc.sync.dma_start(target_sb[:], target.rearrange("(p r) i -> p r i", r=PACK))
+        for h in range(2):
+            nc.sync.dma_start(qrows_sb[h][:], qrows_v[:, :, h * (D // 2) : (h + 1) * (D // 2)])
+        for j in range(PACK):
+            nc.sync.dma_start(old_sb[j][:], old[j * P : (j + 1) * P, :])
+
+        ident = held.tile([P, P], F32, name="ident")
+        make_identity(nc, ident[:])
+        windows = [[held.tile([P, T], F32, name=f"window{l}_{b}") for b in range(2)] for l in range(2)]
+        for l in range(2):
+            for b in range(2):
+                nc.vector.memset(windows[l][b][:], 0.0)
+
+        def turn(dst, src, start=True, stop=True):
+            nc.tensor.matmul(dst, lhsT=src, rhs=ident[:], is_transpose=True, start=start, stop=stop)
+
+        m = held.tile([P, 2, I], F32, name="m")
+        for l in range(2):
+            nc.vector.tensor_copy(m[:, l, :], mass_sb[:].indirect(lists[l][:]))
+        joint_t = ps_small.tile([P, 2, HALF], F32, tag="small", name="joint_t")
+        for h in range(2):
+            for l in range(2):
+                turn(joint_t[:, h, :], m[:, l, h * HALF : (h + 1) * HALF], start=(l == 0), stop=(l == 1))
+
+        part1 = held.tile([P, PACK, I], F32, name="part1")
+        part2 = held.tile([P, PACK, I], F32, name="part2")
+        diff = held.tile([P, EARLY, I], F32, name="diff")
+
+        def gather_early(t):
+            nc.vector.tensor_copy(part2[:, t, :], key_planes[t][:].indirect(list2[:]))
+            nc.vector.tensor_tensor(diff[:, t, :], key_planes[t][:].indirect(list1[:]), part2[:, t, :], ALU.subtract)
+
+        gather_early(0)
+        inv_col = held.tile([P, 2], F32, name="inv_col")
+        nc.vector.reciprocal(inv_col[:], joint_t[:, :, 0])
+        inv_row = ps_small.tile([P, I], F32, tag="small", name="inv_row")
+        for h in range(2):
+            turn(inv_row[:, h * HALF : (h + 1) * HALF], inv_col[:, h : h + 1].to_broadcast([P, P]))
+        gather_early(1)
+        share = held.tile([P, 2, I], F32, name="share")
+        nc.vector.tensor_tensor(share[:], m[:], inv_row[:].unsqueeze(1).to_broadcast([P, 2, I]), ALU.mult)
+        log_inv = held.tile([P, I], F32, name="log_inv")
+        nc.scalar.activation(log_inv[:], inv_row[:], ACT.Ln)
+        for t in range(EARLY, PACK):
+            nc.vector.tensor_tensor(part1[:, t, :], key_planes[t][:].indirect(list1[:]), share[:, 0, :], ALU.mult)
+            nc.vector.tensor_tensor(part2[:, t, :], key_planes[t][:].indirect(list2[:]), share[:, 1, :], ALU.mult)
+        nc.vector.tensor_tensor(
+            part1[:, 0:EARLY, :], diff[:], share[:, 0, :].unsqueeze(1).to_broadcast([P, EARLY, I]), ALU.mult
+        )
+
+        query_g = held.tile([P, PACK, P, PACK], BF16, name="query_g", align_bytes=64)
+        for h in range(2):
+            nc.scalar.copy(
+                query_g[:, :, h * 64 : (h + 1) * 64, :].rearrange("p r s j -> p s j r"),
+                query_sb[h][:].rearrange("p j (s r) -> p s j r", r=PACK),
+            )
+        query_codes = held.tile([P, Q], U32, name="query_codes", align_bytes=64)
+        query_scales = held.tile([P, Q], U8, name="query_scales", align_bytes=64)
+
+        km_g = held.tile([P, I * PACK], BF16, name="km_g", align_bytes=64)
+        km_codes = held.tile([P, I], U32, name="km_codes", align_bytes=64)
+        km_scales = held.tile([P, I], U8, name="km_scales", align_bytes=64)
+
+        def woven(tile, h):
+            return tile[:, h * HALF * PACK : (h + 1) * HALF * PACK].rearrange("p (c i t) -> p c t i", i=4, t=PACK)
+
+        def planes(tile, h):
+            return tile[:, :, h * HALF : (h + 1) * HALF].rearrange("p t (c i) -> p c t i", i=4)
+
+        def quantize_half(codes, scales, grouped, h):
+            cols = slice(h * HALF, (h + 1) * HALF)
+            nc.vector.quantize_mx(
+                out=codes[:, cols].bitcast(FP8X4),
+                scales=scales[:, cols],
+                in_=grouped[:, h * HALF * PACK : (h + 1) * HALF * PACK],
+            )
+
+        for h in range(2):
+            nc.vector.tensor_tensor(woven(km_g, h), planes(part1, h), planes(part2, h), ALU.add)
+        nc.vector.quantize_mx(
+            out=query_codes[:].bitcast(FP8X4),
+            scales=query_scales[:],
+            in_=query_g[:].rearrange("p r s j -> p (r s j)"),
+        )
+        for h in range(2):
+            quantize_half(km_codes, km_scales, km_g, h)
+
+        s = held.tile([P, PACK, I], F32, name="s")
+        for h in range(2):
+            cols = slice(h * HALF, (h + 1) * HALF)
+            a = ps_small.tile([P, PACK, HALF], F32, tag="small", name="a")
+            for r in range(PACK):
+                nc.tensor.matmul_mx(
+                    out=a[:, r, :],
+                    lhsT=query_codes[:, r * P : (r + 1) * P].bitcast(FP8X4),
+                    lhsT_scale=query_scales[:, r * P : (r + 1) * P],
+                    rhs=km_codes[:, cols].bitcast(FP8X4),
+                    rhs_scale=km_scales[:, cols],
+                    start=True,
+                    stop=True,
+                )
+            nc.vector.tensor_tensor(
+                s[:, :, cols], a[:], log_inv[:, cols].unsqueeze(1).to_broadcast([P, PACK, HALF]), ALU.subtract
+            )
+
+        scaled_target = held.tile([P, PACK, I], F32, name="scaled_target")
+        for r in range(PACK):
+            nc.scalar.activation(scaled_target[:, r, :], target_sb[:, r, :], ACT.Copy, scale=qs_sb[:, r : r + 1])
+
+        qrows_g = held.tile([P, D * PACK], BF16, name="qrows_g", align_bytes=64)
+        for h in range(2):
+            nc.scalar.copy(
+                qrows_g[:, h * (D // 2) * PACK : (h + 1) * (D // 2) * PACK].rearrange(
+                    "p (c i j) -> p c j i", i=4, j=PACK
+                ),
+                qrows_sb[h][:].rearrange("p j (c i) -> p c j i", i=4),
+            )
+        qrows_codes = held.tile([P, D], U32, name="qrows_codes", align_bytes=64)
+        qrows_scales = held.tile([P, D], U8, name="qrows_scales", align_bytes=64)
+
+        neg_max = held.tile([P, PACK], F32, name="neg_max")
+        row_sum = held.tile([P, PACK], F32, name="row_sum")
+        inv_sum = held.tile([P, PACK], F32, name="inv_sum")
+        factor = held.tile([P, PACK], F32, name="factor")
+        p = held.tile([P, PACK, I], F32, name="p")
+        ds = held.tile([P, PACK, I], BF16, name="ds")
+        pairs = [slice(0, 2), slice(2, 4)]
+        for pair in pairs:
+            nc.vector.tensor_reduce(neg_max[:, pair], s[:, pair, :], AX.X, ALU.max, negate=True)
+            for r in range(pair.start, pair.stop):
+                nc.scalar.activation(
+                    p[:, r, :], s[:, r, :], ACT.Exp, bias=neg_max[:, r : r + 1], accum_out=row_sum[:, r : r + 1]
+                )
+        for pair in pairs:
+            nc.vector.reciprocal(inv_sum[:, pair], row_sum[:, pair])
+            nc.vector.tensor_tensor(factor[:, pair], inv_sum[:, pair], qs_sb[:, pair], ALU.mult)
+            for r in range(pair.start, pair.stop):
+                nc.vector.scalar_tensor_tensor(
+                    ds[:, r, :], p[:, r, :], factor[:, r : r + 1], scaled_target[:, r, :], ALU.mult, ALU.subtract
+                )
+        nc.vector.quantize_mx(out=qrows_codes[:].bitcast(FP8X4), scales=qrows_scales[:], in_=qrows_g[:])
+
+        ds_g = held.tile([P, I * PACK], BF16, name="ds_g", align_bytes=64)
+        ds_codes = held.tile([P, I], U32, name="ds_codes", align_bytes=64)
+        ds_scales = held.tile([P, I], U8, name="ds_scales", align_bytes=64)
+        for h in range(2):
+            nc.vector.tensor_copy(woven(ds_g, h), planes(ds, h))
+        for h in range(2):
+            quantize_half(ds_codes, ds_scales, ds_g, h)
+
+        sums = {}
+
+        def add_turned(j, src, first, last):
+            for u in range(2):
+                if first:
+                    sums[j, u] = ps_sum.tile([P, PACK, P], F32, tag="sum", name="sum_t")
+                for b in range(PACK):
+                    c0 = u * BANK + b * P
+                    turn(sums[j, u][:, b, :], src[:, c0 : c0 + P], start=(first and b == 0), stop=(last and b == PACK - 1))
+
+        for j in range(3):
+            add_turned(j, old_sb[j], True, False)
+
+        gk = held.tile([P, PACK, I], F32, name="gk")
+        for h in range(2):
+            cols = slice(h * HALF, (h + 1) * HALF)
+            g = ps_small.tile([P, PACK, HALF], F32, tag="small", name="g")
+            for j in range(PACK):
+                nc.tensor.matmul_mx(
+                    out=g[:, j, :],
+                    lhsT=qrows_codes[:, j * P : (j + 1) * P].bitcast(FP8X4),
+                    lhsT_scale=qrows_scales[:, j * P : (j + 1) * P],
+                    rhs=ds_codes[:, cols].bitcast(FP8X4),
+                    rhs_scale=ds_scales[:, cols],
+                    start=True,
+                    stop=True,
+                )
+            nc.scalar.copy(gk[:, 0, cols], g[:, 0, :])
+            nc.scalar.copy(gk[:, 1:PACK, cols], g[:, 1:PACK, :])
+
+        def scatter(j, l, window):
+            nc.vector.tensor_tensor(window[:].indirect(lists[l][:]), gk[:, j, :], share[:, l, :], ALU.mult)
+
+        def turn_back(j, res):
+            for u in range(2):
+                staged = ring.tile([P, PACK, P], F32, tag="staged", name="staged")
+                nc.scalar.copy(staged[:], sums[j, u][:])
+                back = ps_small.tile([P, PACK, P], F32, tag="small", name="back")
+                for b in range(PACK):
+                    turn(back[:, b, :], staged[:, b, :])
+                nc.scalar.copy(res[:, u * BANK : (u + 1) * BANK], back[:].rearrange("p b t -> p (b t)"))
+
+        results = [held.tile([P, T], F32, name=f"result{j}") for j in range(PACK)]
+        for h in range(2):
+            cols = slice(h * HALF, (h + 1) * HALF)
+            nc.vector.tensor_tensor(
+                windows[0][0][:].indirect(list1[:, h * 8 : (h + 1) * 8]), gk[:, 0, cols], share[:, 0, cols], ALU.mult
+            )
+        add_turned(0, windows[0][0], False, True)
+        turn_back(0, results[0])
+        for j in (1, 2):
+            scatter(j, 0, windows[0][j % 2])
+            add_turned(j, windows[0][j % 2], False, False)
+            scatter(j, 1, windows[1][j % 2])
+            add_turned(j, windows[1][j % 2], False, True)
+            turn_back(j, results[j])
+            nc.sync.dma_start(out[j * P : (j + 1) * P, :], results[j][:])
+        add_turned(3, old_sb[3], True, False)
+        scatter(3, 0, windows[0][1])
+        add_turned(3, windows[0][1], False, True)
+        turn_back(3, results[3])
+        for j in (0, 3):
+            window = windows[1][(j + 1) % 2]
+            scatter(j, 1, window)
+            last = held.tile([P, T], F32, name=f"last{j}")
+            for u in range(2):
+                cols = slice(u * BANK, (u + 1) * BANK)
+                nc.vector.tensor_tensor(last[:, cols], results[j][:, cols], window[:, cols], ALU.add)
+                nc.sync.dma_start(out[j * P : (j + 1) * P, cols], last[:, cols])

@@ -28,8 +28,9 @@ def tile_attend_bmassmerge_kernel(tc, query, keys, mass, target, qs, qrows, old,
     with ExitStack() as ctx:
         held = ctx.enter_context(tc.tile_pool(name="held", bufs=1))
         ring = ctx.enter_context(tc.tile_pool(name="ring", bufs=3))
-        ps_small = ctx.enter_context(tc.psum_pool(name="ps_small", bufs=2))
-        ps_sum = ctx.enter_context(tc.psum_pool(name="ps_sum", bufs=6))
+        psum = ctx.enter_context(tc.psum_pool(name="psum", bufs=1))
+        banks = [[psum.tile([P, PACK, P], F32, name=f"bank{j}_{u}") for u in range(2)] for j in range(PACK)]
+        early_banks = banks[PACK - 1]
 
         list1 = held.tile([P, I // 16], U16, name="list1")
         list2 = held.tile([P, I // 16], U16, name="list2")
@@ -63,10 +64,10 @@ def tile_attend_bmassmerge_kernel(tc, query, keys, mass, target, qs, qrows, old,
 
         ident = held.tile([P, P], F32, name="ident")
         make_identity(nc, ident[:])
-        windows = [[held.tile([P, T], F32, name=f"window{l}_{b}") for b in range(2)] for l in range(2)]
-        for l in range(2):
-            for b in range(2):
-                nc.vector.memset(windows[l][b][:], 0.0)
+        windows = [[held.tile([P, T], F32, name=f"window{l}_{b}") for b in range(2 - l)] for l in range(2)]
+        nc.vector.memset(windows[0][0][:], 0.0)
+        nc.vector.memset(windows[1][0][:], 0.0)
+        nc.gpsimd.memset(windows[0][1][:], 0.0)
 
         def turn(dst, src, start=True, stop=True):
             nc.tensor.matmul(dst, lhsT=src, rhs=ident[:], is_transpose=True, start=start, stop=stop)
@@ -74,7 +75,7 @@ def tile_attend_bmassmerge_kernel(tc, query, keys, mass, target, qs, qrows, old,
         m = held.tile([P, 2, I], F32, name="m")
         for l in range(2):
             nc.vector.tensor_copy(m[:, l, :], mass_sb[:].indirect(lists[l][:]))
-        joint_t = ps_small.tile([P, 2, HALF], F32, tag="small", name="joint_t")
+        joint_t = early_banks[0]
         for h in range(2):
             for l in range(2):
                 turn(joint_t[:, h, :], m[:, l, h * HALF : (h + 1) * HALF], start=(l == 0), stop=(l == 1))
@@ -89,15 +90,15 @@ def tile_attend_bmassmerge_kernel(tc, query, keys, mass, target, qs, qrows, old,
 
         gather_early(0)
         inv_col = held.tile([P, 2], F32, name="inv_col")
-        nc.vector.reciprocal(inv_col[:], joint_t[:, :, 0])
-        inv_row = ps_small.tile([P, I], F32, tag="small", name="inv_row")
+        nc.vector.reciprocal(inv_col[:], joint_t[:, 0:2, 0])
+        inv_row = early_banks[1][:, 0:2, :].rearrange("p h i -> p (h i)")
         for h in range(2):
             turn(inv_row[:, h * HALF : (h + 1) * HALF], inv_col[:, h : h + 1].to_broadcast([P, P]))
         gather_early(1)
         share = held.tile([P, 2, I], F32, name="share")
-        nc.vector.tensor_tensor(share[:], m[:], inv_row[:].unsqueeze(1).to_broadcast([P, 2, I]), ALU.mult)
+        nc.vector.tensor_tensor(share[:], m[:], inv_row.unsqueeze(1).to_broadcast([P, 2, I]), ALU.mult)
         log_inv = held.tile([P, I], F32, name="log_inv")
-        nc.scalar.activation(log_inv[:], inv_row[:], ACT.Ln)
+        nc.scalar.activation(log_inv[:], inv_row, ACT.Ln)
         for t in range(EARLY, PACK):
             nc.vector.tensor_tensor(part1[:, t, :], key_planes[t][:].indirect(list1[:]), share[:, 0, :], ALU.mult)
             nc.vector.tensor_tensor(part2[:, t, :], key_planes[t][:].indirect(list2[:]), share[:, 1, :], ALU.mult)
@@ -132,33 +133,36 @@ def tile_attend_bmassmerge_kernel(tc, query, keys, mass, target, qs, qrows, old,
                 in_=grouped[:, h * HALF * PACK : (h + 1) * HALF * PACK],
             )
 
-        for h in range(2):
-            nc.vector.tensor_tensor(woven(km_g, h), planes(part1, h), planes(part2, h), ALU.add)
+        nc.vector.tensor_tensor(
+            km_g[:].rearrange("p (c i t) -> p c t i", i=4, t=PACK),
+            part1[:].rearrange("p t (c i) -> p c t i", i=4),
+            part2[:].rearrange("p t (c i) -> p c t i", i=4),
+            ALU.add,
+        )
         nc.vector.quantize_mx(
             out=query_codes[:].bitcast(FP8X4),
             scales=query_scales[:],
             in_=query_g[:].rearrange("p r s j -> p (r s j)"),
         )
-        for h in range(2):
-            quantize_half(km_codes, km_scales, km_g, h)
+        nc.vector.quantize_mx(out=km_codes[:].bitcast(FP8X4), scales=km_scales[:], in_=km_g[:])
 
         s = held.tile([P, PACK, I], F32, name="s")
-        for h in range(2):
-            cols = slice(h * HALF, (h + 1) * HALF)
-            a = ps_small.tile([P, PACK, HALF], F32, tag="small", name="a")
-            for r in range(PACK):
+        neg_max = held.tile([P, PACK], F32, name="neg_max")
+        pairs = [slice(0, 2), slice(2, 4)]
+        for u, pair in enumerate(pairs):
+            a = early_banks[u][:].rearrange("p (r h) i -> p r (h i)", r=2)
+            for r in range(pair.start, pair.stop):
                 nc.tensor.matmul_mx(
-                    out=a[:, r, :],
+                    out=a[:, r - pair.start, :],
                     lhsT=query_codes[:, r * P : (r + 1) * P].bitcast(FP8X4),
                     lhsT_scale=query_scales[:, r * P : (r + 1) * P],
-                    rhs=km_codes[:, cols].bitcast(FP8X4),
-                    rhs_scale=km_scales[:, cols],
+                    rhs=km_codes[:].bitcast(FP8X4),
+                    rhs_scale=km_scales[:],
                     start=True,
                     stop=True,
                 )
-            nc.vector.tensor_tensor(
-                s[:, :, cols], a[:], log_inv[:, cols].unsqueeze(1).to_broadcast([P, PACK, HALF]), ALU.subtract
-            )
+            nc.vector.tensor_tensor(s[:, pair, :], a, log_inv[:].unsqueeze(1).to_broadcast([P, 2, I]), ALU.subtract)
+            nc.vector.tensor_reduce(neg_max[:, pair], s[:, pair, :], AX.X, ALU.max, negate=True)
 
         scaled_target = held.tile([P, PACK, I], F32, name="scaled_target")
         for r in range(PACK):
@@ -175,56 +179,49 @@ def tile_attend_bmassmerge_kernel(tc, query, keys, mass, target, qs, qrows, old,
         qrows_codes = held.tile([P, D], U32, name="qrows_codes", align_bytes=64)
         qrows_scales = held.tile([P, D], U8, name="qrows_scales", align_bytes=64)
 
-        neg_max = held.tile([P, PACK], F32, name="neg_max")
         row_sum = held.tile([P, PACK], F32, name="row_sum")
         inv_sum = held.tile([P, PACK], F32, name="inv_sum")
         factor = held.tile([P, PACK], F32, name="factor")
         p = held.tile([P, PACK, I], F32, name="p")
         ds = held.tile([P, PACK, I], BF16, name="ds")
-        pairs = [slice(0, 2), slice(2, 4)]
-        for pair in pairs:
-            nc.vector.tensor_reduce(neg_max[:, pair], s[:, pair, :], AX.X, ALU.max, negate=True)
-            for r in range(pair.start, pair.stop):
-                nc.scalar.activation(
-                    p[:, r, :], s[:, r, :], ACT.Exp, bias=neg_max[:, r : r + 1], accum_out=row_sum[:, r : r + 1]
-                )
+        for r in range(PACK):
+            nc.scalar.activation(
+                p[:, r, :], s[:, r, :], ACT.Exp, bias=neg_max[:, r : r + 1], accum_out=row_sum[:, r : r + 1]
+            )
         for pair in pairs:
             nc.vector.reciprocal(inv_sum[:, pair], row_sum[:, pair])
             nc.vector.tensor_tensor(factor[:, pair], inv_sum[:, pair], qs_sb[:, pair], ALU.mult)
-            for r in range(pair.start, pair.stop):
-                nc.vector.scalar_tensor_tensor(
-                    ds[:, r, :], p[:, r, :], factor[:, r : r + 1], scaled_target[:, r, :], ALU.mult, ALU.subtract
-                )
+        for r in range(PACK):
+            nc.vector.scalar_tensor_tensor(
+                ds[:, r, :], p[:, r, :], factor[:, r : r + 1], scaled_target[:, r, :], ALU.mult, ALU.subtract
+            )
         nc.vector.quantize_mx(out=qrows_codes[:].bitcast(FP8X4), scales=qrows_scales[:], in_=qrows_g[:])
 
         ds_g = held.tile([P, I * PACK], BF16, name="ds_g", align_bytes=64)
-        ds_codes = held.tile([P, I], U32, name="ds_codes", align_bytes=64)
-        ds_scales = held.tile([P, I], U8, name="ds_scales", align_bytes=64)
-        for h in range(2):
-            nc.vector.tensor_copy(woven(ds_g, h), planes(ds, h))
+        ds_codes = held.tile([P, I], U32, tag="late0", name="ds_codes", align_bytes=64)
+        ds_scales = held.tile([P, I], U8, tag="late1", name="ds_scales", align_bytes=64)
+        nc.vector.tensor_copy(woven(ds_g, 0), planes(ds, 0))
+        nc.scalar.copy(woven(ds_g, 1), planes(ds, 1))
         for h in range(2):
             quantize_half(ds_codes, ds_scales, ds_g, h)
 
-        sums = {}
-
         def add_turned(j, src, first, last):
             for u in range(2):
-                if first:
-                    sums[j, u] = ps_sum.tile([P, PACK, P], F32, tag="sum", name="sum_t")
                 for b in range(PACK):
                     c0 = u * BANK + b * P
-                    turn(sums[j, u][:, b, :], src[:, c0 : c0 + P], start=(first and b == 0), stop=(last and b == PACK - 1))
+                    turn(banks[j][u][:, b, :], src[:, c0 : c0 + P], start=(first and b == 0), stop=(last and b == PACK - 1))
 
         for j in range(3):
             add_turned(j, old_sb[j], True, False)
 
-        gk = held.tile([P, PACK, I], F32, name="gk")
-        for h in range(2):
-            cols = slice(h * HALF, (h + 1) * HALF)
-            g = ps_small.tile([P, PACK, HALF], F32, tag="small", name="g")
-            for j in range(PACK):
+        gk = held.tile([P, PACK * I], F32, name="gk")
+
+        def key_gradient(bank, pieces):
+            flat = bank[:].rearrange("p b i -> p (b i)")
+            first = pieces[0][0] * I + pieces[0][1].start
+            for j, cols in pieces:
                 nc.tensor.matmul_mx(
-                    out=g[:, j, :],
+                    out=flat[:, j * I + cols.start - first : j * I + cols.stop - first],
                     lhsT=qrows_codes[:, j * P : (j + 1) * P].bitcast(FP8X4),
                     lhsT_scale=qrows_scales[:, j * P : (j + 1) * P],
                     rhs=ds_codes[:, cols].bitcast(FP8X4),
@@ -232,45 +229,59 @@ def tile_attend_bmassmerge_kernel(tc, query, keys, mass, target, qs, qrows, old,
                     start=True,
                     stop=True,
                 )
-            nc.scalar.copy(gk[:, 0, cols], g[:, 0, :])
-            nc.scalar.copy(gk[:, 1:PACK, cols], g[:, 1:PACK, :])
+            for j, cols in pieces:
+                nc.scalar.copy(
+                    gk[:, j * I + cols.start : j * I + cols.stop],
+                    flat[:, j * I + cols.start - first : j * I + cols.stop - first],
+                )
+
+        key_gradient(early_banks[0], [(0, slice(0, HALF))])
+        key_gradient(early_banks[1], [(0, slice(HALF, I)), (1, slice(0, I))])
+        key_gradient(early_banks[0], [(2, slice(0, I)), (3, slice(0, I))])
+
+        for l in (1, 0):
+            window = held.tile([P, T], F32, tag=f"late{l}", name=f"late_window{l}", align_bytes=64)
+            nc.gpsimd.memset(window[:], 0.0)
+            windows[l].append(window)
 
         def scatter(j, l, window):
-            nc.vector.tensor_tensor(window[:].indirect(lists[l][:]), gk[:, j, :], share[:, l, :], ALU.mult)
+            nc.vector.tensor_tensor(window[:].indirect(lists[l][:]), gk[:, j * I : (j + 1) * I], share[:, l, :], ALU.mult)
 
-        def turn_back(j, res):
+        def turn_back(j):
             for u in range(2):
                 staged = ring.tile([P, PACK, P], F32, tag="staged", name="staged")
-                nc.scalar.copy(staged[:], sums[j, u][:])
-                back = ps_small.tile([P, PACK, P], F32, tag="small", name="back")
+                nc.scalar.copy(staged[:], banks[j][u][:])
                 for b in range(PACK):
-                    turn(back[:, b, :], staged[:, b, :])
-                nc.scalar.copy(res[:, u * BANK : (u + 1) * BANK], back[:].rearrange("p b t -> p (b t)"))
+                    turn(banks[j][u][:, b, :], staged[:, b, :])
 
-        results = [held.tile([P, T], F32, name=f"result{j}") for j in range(PACK)]
-        for h in range(2):
-            cols = slice(h * HALF, (h + 1) * HALF)
-            nc.vector.tensor_tensor(
-                windows[0][0][:].indirect(list1[:, h * 8 : (h + 1) * 8]), gk[:, 0, cols], share[:, 0, cols], ALU.mult
-            )
-        add_turned(0, windows[0][0], False, True)
-        turn_back(0, results[0])
-        for j in (1, 2):
-            scatter(j, 0, windows[0][j % 2])
-            add_turned(j, windows[0][j % 2], False, False)
-            scatter(j, 1, windows[1][j % 2])
-            add_turned(j, windows[1][j % 2], False, True)
-            turn_back(j, results[j])
-            nc.sync.dma_start(out[j * P : (j + 1) * P, :], results[j][:])
         add_turned(3, old_sb[3], True, False)
-        scatter(3, 0, windows[0][1])
-        add_turned(3, windows[0][1], False, True)
-        turn_back(3, results[3])
-        for j in (0, 3):
-            window = windows[1][(j + 1) % 2]
+        results = [held.tile([P, T], F32, name=f"result{j}") for j in range(PACK)]
+        for j in (0, 1):
+            if j == 0:
+                for h in range(2):
+                    cols = slice(h * HALF, (h + 1) * HALF)
+                    nc.vector.tensor_tensor(
+                        windows[0][0][:].indirect(list1[:, h * 8 : (h + 1) * 8]), gk[:, cols], share[:, 0, cols], ALU.mult
+                    )
+            else:
+                scatter(j, 0, windows[0][j])
+            add_turned(j, windows[0][j], False, False)
+            scatter(j, 1, windows[1][j])
+            add_turned(j, windows[1][j], False, True)
+            turn_back(j)
+            for u in range(2):
+                nc.scalar.copy(results[j][:, u * BANK : (u + 1) * BANK], banks[j][u][:].rearrange("p b t -> p (b t)"))
+            nc.sync.dma_start(out[j * P : (j + 1) * P, :], results[j][:])
+        for j in (2, 3):
+            scatter(j, 0, windows[0][j % 3])
+            add_turned(j, windows[0][j % 3], False, True)
+            turn_back(j)
+        for j in (2, 3):
+            window = windows[1][j % 2]
             scatter(j, 1, window)
-            last = held.tile([P, T], F32, name=f"last{j}")
             for u in range(2):
                 cols = slice(u * BANK, (u + 1) * BANK)
-                nc.vector.tensor_tensor(last[:, cols], results[j][:, cols], window[:, cols], ALU.add)
-                nc.sync.dma_start(out[j * P : (j + 1) * P, cols], last[:, cols])
+                nc.vector.tensor_tensor(
+                    results[j][:, cols], banks[j][u][:].rearrange("p b t -> p (b t)"), window[:, cols], ALU.add
+                )
+                nc.sync.dma_start(out[j * P : (j + 1) * P, cols], results[j][:, cols])

@@ -36,12 +36,11 @@ def tile_attend_bmassmerge_kernel(tc, query, keys, mass, target, qs, qrows, old,
         list2 = held.tile([P, I // 16], U16, name="list2")
         lists = (list1, list2)
         mass_sb = held.tile([P, T], F32, name="mass_sb")
-        key_planes = [held.tile([P, T], F32, name=f"key_plane{t}") for t in range(PACK)]
+        key_planes = [held.tile([P, T], F32, tag=f"key_plane{t}", name=f"key_plane{t}") for t in range(PACK)]
         query_sb = [held.tile([P, PACK, Q // 2], F32, name=f"query_sb{h}") for h in range(2)]
         qrows_sb = [held.tile([P, PACK, D // 2], F32, name=f"qrows_sb{h}") for h in range(2)]
         target_sb = held.tile([P, PACK, I], F32, name="target_sb")
         qs_sb = held.tile([P, PACK], F32, name="qs_sb")
-        old_sb = [held.tile([P, T], F32, name=f"old_sb{j}") for j in range(PACK)]
 
         keys_v = keys.rearrange("(p t) n -> p t n", t=PACK)
         query_v = query.rearrange("(p j) q -> p j q", j=PACK)
@@ -49,25 +48,22 @@ def tile_attend_bmassmerge_kernel(tc, query, keys, mass, target, qs, qrows, old,
         nc.sync.dma_start(mass_sb[:], mass)
         nc.sync.dma_start(list1[:], offs)
         nc.sync.dma_start(list2[:], offs2)
-        nc.sync.dma_start(key_planes[0][:], keys_v[:, 0, :])
-        nc.sync.dma_start(key_planes[1][:], keys_v[:, 1, :])
-        nc.sync.dma_start(query_sb[0][:], query_v[:, :, 0 : Q // 2])
-        nc.sync.dma_start(key_planes[2][:], keys_v[:, 2, :])
-        nc.sync.dma_start(key_planes[3][:], keys_v[:, 3, :])
-        nc.sync.dma_start(query_sb[1][:], query_v[:, :, Q // 2 : Q])
+        for t in range(PACK):
+            nc.sync.dma_start(key_planes[t][:], keys_v[:, t, :])
+        for h in range(2):
+            nc.sync.dma_start(query_sb[h][:], query_v[:, :, h * (Q // 2) : (h + 1) * (Q // 2)])
         nc.sync.dma_start(qs_sb[:], qs.rearrange("(p r) o -> p (r o)", r=PACK))
         nc.sync.dma_start(target_sb[:], target.rearrange("(p r) i -> p r i", r=PACK))
         for h in range(2):
             nc.sync.dma_start(qrows_sb[h][:], qrows_v[:, :, h * (D // 2) : (h + 1) * (D // 2)])
-        for j in range(PACK):
-            nc.sync.dma_start(old_sb[j][:], old[j * P : (j + 1) * P, :])
 
         ident = held.tile([P, P], F32, name="ident")
         make_identity(nc, ident[:])
-        windows = [[held.tile([P, T], F32, name=f"window{l}_{b}") for b in range(2 - l)] for l in range(2)]
+        windows = [[held.tile([P, T], F32, name=f"window{l}_{b}") for b in range(2)] for l in range(2)]
         nc.vector.memset(windows[0][0][:], 0.0)
+        nc.vector.memset(windows[0][1][:], 0.0)
         nc.vector.memset(windows[1][0][:], 0.0)
-        nc.gpsimd.memset(windows[0][1][:], 0.0)
+        nc.gpsimd.memset(windows[1][1][:], 0.0)
 
         def turn(dst, src, start=True, stop=True):
             nc.tensor.matmul(dst, lhsT=src, rhs=ident[:], is_transpose=True, start=start, stop=stop)
@@ -80,9 +76,9 @@ def tile_attend_bmassmerge_kernel(tc, query, keys, mass, target, qs, qrows, old,
             for l in range(2):
                 turn(joint_t[:, h, :], m[:, l, h * HALF : (h + 1) * HALF], start=(l == 0), stop=(l == 1))
 
-        part1 = held.tile([P, PACK, I], F32, name="part1")
-        part2 = held.tile([P, PACK, I], F32, name="part2")
-        diff = held.tile([P, EARLY, I], F32, name="diff")
+        part1 = held.tile([P, PACK, I], F32, tag="part1", name="part1")
+        part2 = held.tile([P, PACK, I], F32, tag="part2", name="part2")
+        diff = held.tile([P, EARLY, I], F32, tag="diff", name="diff", align_bytes=64)
 
         def gather_early(t):
             nc.vector.tensor_copy(part2[:, t, :], key_planes[t][:].indirect(list2[:]))
@@ -90,15 +86,23 @@ def tile_attend_bmassmerge_kernel(tc, query, keys, mass, target, qs, qrows, old,
 
         gather_early(0)
         inv_col = held.tile([P, 2], F32, name="inv_col")
-        nc.vector.reciprocal(inv_col[:], joint_t[:, 0:2, 0])
+        joint_col = part2[:, 1, 0:2]
+        log_col = held.tile([P, 2], F32, name="log_col")
+        nc.scalar.activation(log_col[:], joint_t[:, 0:2, 0], ACT.Ln)
+        nc.scalar.copy(joint_col, joint_t[:, 0:2, 0])
+        nc.vector.reciprocal(inv_col[:], joint_col)
         inv_row = early_banks[1][:, 0:2, :].rearrange("p h i -> p (h i)")
         for h in range(2):
             turn(inv_row[:, h * HALF : (h + 1) * HALF], inv_col[:, h : h + 1].to_broadcast([P, P]))
         gather_early(1)
         share = held.tile([P, 2, I], F32, name="share")
         nc.vector.tensor_tensor(share[:], m[:], inv_row.unsqueeze(1).to_broadcast([P, 2, I]), ALU.mult)
-        log_inv = held.tile([P, I], F32, name="log_inv")
-        nc.scalar.activation(log_inv[:], inv_row, ACT.Ln)
+        log_row = held.tile([P, I], F32, name="log_row")
+        for h in range(2):
+            turn(joint_t[:, 2 + h, :], log_col[:, h : h + 1].to_broadcast([P, P]))
+        nc.scalar.copy(log_row[:], joint_t[:, 2:4, :].rearrange("p h i -> p (h i)"))
+        warm = held.tile([P, 1], F32, name="warm")
+        nc.scalar.activation(warm[:], log_row[:, 0:1], ACT.Exp)
         for t in range(EARLY, PACK):
             nc.vector.tensor_tensor(part1[:, t, :], key_planes[t][:].indirect(list1[:]), share[:, 0, :], ALU.mult)
             nc.vector.tensor_tensor(part2[:, t, :], key_planes[t][:].indirect(list2[:]), share[:, 1, :], ALU.mult)
@@ -112,10 +116,10 @@ def tile_attend_bmassmerge_kernel(tc, query, keys, mass, target, qs, qrows, old,
                 query_g[:, :, h * 64 : (h + 1) * 64, :].rearrange("p r s j -> p s j r"),
                 query_sb[h][:].rearrange("p j (s r) -> p s j r", r=PACK),
             )
-        query_codes = held.tile([P, Q], U32, name="query_codes", align_bytes=64)
+        query_codes = held.tile([P, Q], U32, tag="diff", name="query_codes", align_bytes=64)
         query_scales = held.tile([P, Q], U8, name="query_scales", align_bytes=64)
 
-        km_g = held.tile([P, I * PACK], BF16, name="km_g", align_bytes=64)
+        km_g = held.tile([P, I * PACK], BF16, tag="km_g", name="km_g", align_bytes=64)
         km_codes = held.tile([P, I], U32, name="km_codes", align_bytes=64)
         km_scales = held.tile([P, I], U8, name="km_scales", align_bytes=64)
 
@@ -146,7 +150,12 @@ def tile_attend_bmassmerge_kernel(tc, query, keys, mass, target, qs, qrows, old,
         )
         nc.vector.quantize_mx(out=km_codes[:].bitcast(FP8X4), scales=km_scales[:], in_=km_g[:])
 
-        s = held.tile([P, PACK, I], F32, name="s")
+        old_sb = []
+        for j, freed in enumerate(("key_plane3", "part1", "part2", "key_plane2")):
+            old_sb.append(held.tile([P, T], F32, tag=freed, name=f"old_sb{j}"))
+            nc.sync.dma_start(old_sb[j][:], old[j * P : (j + 1) * P, :])
+
+        s = held.tile([P, PACK, I], F32, tag="scores", name="s", align_bytes=64)
         neg_max = held.tile([P, PACK], F32, name="neg_max")
         pairs = [slice(0, 2), slice(2, 4)]
         for u, pair in enumerate(pairs):
@@ -161,49 +170,56 @@ def tile_attend_bmassmerge_kernel(tc, query, keys, mass, target, qs, qrows, old,
                     start=True,
                     stop=True,
                 )
-            nc.vector.tensor_tensor(s[:, pair, :], a, log_inv[:].unsqueeze(1).to_broadcast([P, 2, I]), ALU.subtract)
+            nc.vector.tensor_tensor(s[:, pair, :], a, log_row[:].unsqueeze(1).to_broadcast([P, 2, I]), ALU.add)
             nc.vector.tensor_reduce(neg_max[:, pair], s[:, pair, :], AX.X, ALU.max, negate=True)
 
         scaled_target = held.tile([P, PACK, I], F32, name="scaled_target")
         for r in range(PACK):
             nc.scalar.activation(scaled_target[:, r, :], target_sb[:, r, :], ACT.Copy, scale=qs_sb[:, r : r + 1])
 
-        qrows_g = held.tile([P, D * PACK], BF16, name="qrows_g", align_bytes=64)
-        for h in range(2):
+        qrows_codes = [
+            held.tile([P, D // 2], U32, tag=tag, name=f"qrows_codes{h}", align_bytes=64)
+            for h, tag in enumerate(("km_g", "qrows_codes1"))
+        ]
+        qrows_scales = [held.tile([P, D // 2], U8, name=f"qrows_scales{h}", align_bytes=64) for h in range(2)]
+
+        def weave_qrows(h, grouped):
             nc.scalar.copy(
-                qrows_g[:, h * (D // 2) * PACK : (h + 1) * (D // 2) * PACK].rearrange(
-                    "p (c i j) -> p c j i", i=4, j=PACK
-                ),
+                grouped[:].rearrange("p (c i j) -> p c j i", i=4, j=PACK),
                 qrows_sb[h][:].rearrange("p j (c i) -> p c j i", i=4),
             )
-        qrows_codes = held.tile([P, D], U32, name="qrows_codes", align_bytes=64)
-        qrows_scales = held.tile([P, D], U8, name="qrows_scales", align_bytes=64)
+
+        def quantize_qrows(h, grouped):
+            nc.vector.quantize_mx(out=qrows_codes[h][:].bitcast(FP8X4), scales=qrows_scales[h][:], in_=grouped[:])
+
+        qrows_g0 = held.tile([P, D // 2 * PACK], BF16, name="qrows_g0", align_bytes=64)
+        weave_qrows(0, qrows_g0)
+        quantize_qrows(0, qrows_g0)
 
         row_sum = held.tile([P, PACK], F32, name="row_sum")
         inv_sum = held.tile([P, PACK], F32, name="inv_sum")
-        factor = held.tile([P, PACK], F32, name="factor")
         p = held.tile([P, PACK, I], F32, name="p")
-        ds = held.tile([P, PACK, I], BF16, name="ds")
+        weighted = held.tile([P, PACK, I], F32, name="weighted")
         for r in range(PACK):
             nc.scalar.activation(
                 p[:, r, :], s[:, r, :], ACT.Exp, bias=neg_max[:, r : r + 1], accum_out=row_sum[:, r : r + 1]
             )
+        qrows_g1 = held.tile([P, D // 2 * PACK], BF16, tag="scores", name="qrows_g1", align_bytes=64)
+        weave_qrows(1, qrows_g1)
         for pair in pairs:
             nc.vector.reciprocal(inv_sum[:, pair], row_sum[:, pair])
-            nc.vector.tensor_tensor(factor[:, pair], inv_sum[:, pair], qs_sb[:, pair], ALU.mult)
-        for r in range(PACK):
-            nc.vector.scalar_tensor_tensor(
-                ds[:, r, :], p[:, r, :], factor[:, r : r + 1], scaled_target[:, r, :], ALU.mult, ALU.subtract
-            )
-        nc.vector.quantize_mx(out=qrows_codes[:].bitcast(FP8X4), scales=qrows_scales[:], in_=qrows_g[:])
+            for r in range(pair.start, pair.stop):
+                nc.vector.tensor_scalar(
+                    weighted[:, r, :], p[:, r, :], inv_sum[:, r : r + 1], qs_sb[:, r : r + 1], ALU.mult, ALU.mult
+                )
 
         ds_g = held.tile([P, I * PACK], BF16, name="ds_g", align_bytes=64)
-        ds_codes = held.tile([P, I], U32, tag="late0", name="ds_codes", align_bytes=64)
-        ds_scales = held.tile([P, I], U8, tag="late1", name="ds_scales", align_bytes=64)
-        nc.vector.tensor_copy(woven(ds_g, 0), planes(ds, 0))
-        nc.scalar.copy(woven(ds_g, 1), planes(ds, 1))
+        ds_codes = held.tile([P, I], U32, name="ds_codes", align_bytes=64)
+        ds_scales = held.tile([P, I], U8, name="ds_scales", align_bytes=64)
         for h in range(2):
+            nc.vector.tensor_tensor(woven(ds_g, h), planes(weighted, h), planes(scaled_target, h), ALU.subtract)
             quantize_half(ds_codes, ds_scales, ds_g, h)
+        quantize_qrows(1, qrows_g1)
 
         def add_turned(j, src, first, last):
             for u in range(2):
@@ -222,8 +238,8 @@ def tile_attend_bmassmerge_kernel(tc, query, keys, mass, target, qs, qrows, old,
             for j, cols in pieces:
                 nc.tensor.matmul_mx(
                     out=flat[:, j * I + cols.start - first : j * I + cols.stop - first],
-                    lhsT=qrows_codes[:, j * P : (j + 1) * P].bitcast(FP8X4),
-                    lhsT_scale=qrows_scales[:, j * P : (j + 1) * P],
+                    lhsT=qrows_codes[j // 2][:, j % 2 * P : (j % 2 + 1) * P].bitcast(FP8X4),
+                    lhsT_scale=qrows_scales[j // 2][:, j % 2 * P : (j % 2 + 1) * P],
                     rhs=ds_codes[:, cols].bitcast(FP8X4),
                     rhs_scale=ds_scales[:, cols],
                     start=True,
@@ -239,11 +255,6 @@ def tile_attend_bmassmerge_kernel(tc, query, keys, mass, target, qs, qrows, old,
         key_gradient(early_banks[1], [(0, slice(HALF, I)), (1, slice(0, I))])
         key_gradient(early_banks[0], [(2, slice(0, I)), (3, slice(0, I))])
 
-        for l in (1, 0):
-            window = held.tile([P, T], F32, tag=f"late{l}", name=f"late_window{l}", align_bytes=64)
-            nc.gpsimd.memset(window[:], 0.0)
-            windows[l].append(window)
-
         def scatter(j, l, window):
             nc.vector.tensor_tensor(window[:].indirect(lists[l][:]), gk[:, j * I : (j + 1) * I], share[:, l, :], ALU.mult)
 
@@ -256,27 +267,26 @@ def tile_attend_bmassmerge_kernel(tc, query, keys, mass, target, qs, qrows, old,
 
         add_turned(3, old_sb[3], True, False)
         results = [held.tile([P, T], F32, name=f"result{j}") for j in range(PACK)]
-        for j in (0, 1):
-            if j == 0:
-                for h in range(2):
-                    cols = slice(h * HALF, (h + 1) * HALF)
-                    nc.vector.tensor_tensor(
-                        windows[0][0][:].indirect(list1[:, h * 8 : (h + 1) * 8]), gk[:, cols], share[:, 0, cols], ALU.mult
-                    )
-            else:
-                scatter(j, 0, windows[0][j])
-            add_turned(j, windows[0][j], False, False)
-            scatter(j, 1, windows[1][j])
-            add_turned(j, windows[1][j], False, True)
+        for h in range(2):
+            cols = slice(h * HALF, (h + 1) * HALF)
+            nc.vector.tensor_tensor(
+                windows[0][0][:].indirect(list1[:, h * 8 : (h + 1) * 8]), gk[:, cols], share[:, 0, cols], ALU.mult
+            )
+        add_turned(0, windows[0][0], False, True)
+        turn_back(0)
+        for j, order in ((1, (0, 1)), (2, (1, 0))):
+            for l in order:
+                window = windows[l][(j + l) % 2]
+                scatter(j, l, window)
+                add_turned(j, window, False, l == order[1])
             turn_back(j)
             for u in range(2):
                 nc.scalar.copy(results[j][:, u * BANK : (u + 1) * BANK], banks[j][u][:].rearrange("p b t -> p (b t)"))
-            nc.sync.dma_start(out[j * P : (j + 1) * P, :], results[j][:])
-        for j in (2, 3):
-            scatter(j, 0, windows[0][j % 3])
-            add_turned(j, windows[0][j % 3], False, True)
-            turn_back(j)
-        for j in (2, 3):
+            nc.scalar.dma_start(out[j * P : (j + 1) * P, :], results[j][:])
+        scatter(3, 0, windows[0][1])
+        add_turned(3, windows[0][1], False, True)
+        turn_back(3)
+        for j in (0, 3):
             window = windows[1][j % 2]
             scatter(j, 1, window)
             for u in range(2):

@@ -59,11 +59,10 @@ def tile_attend_bmassmerge_kernel(tc, query, keys, mass, target, qs, qrows, old,
 
         ident = held.tile([P, P], F32, name="ident")
         make_identity(nc, ident[:])
-        windows = [[held.tile([P, T], F32, name=f"window{l}_{b}") for b in range(2)] for l in range(2)]
+        windows = [[held.tile([P, T], F32, name=f"window{l}_{b}") for b in range(2 - l)] for l in range(2)]
         nc.vector.memset(windows[0][0][:], 0.0)
         nc.vector.memset(windows[0][1][:], 0.0)
-        nc.vector.memset(windows[1][0][:], 0.0)
-        nc.gpsimd.memset(windows[1][1][:], 0.0)
+        nc.gpsimd.memset(windows[1][0][:], 0.0)
 
         def turn(dst, src, start=True, stop=True):
             nc.tensor.matmul(dst, lhsT=src, rhs=ident[:], is_transpose=True, start=start, stop=stop)
@@ -101,8 +100,6 @@ def tile_attend_bmassmerge_kernel(tc, query, keys, mass, target, qs, qrows, old,
         for h in range(2):
             turn(joint_t[:, 2 + h, :], log_col[:, h : h + 1].to_broadcast([P, P]))
         nc.scalar.copy(log_row[:], joint_t[:, 2:4, :].rearrange("p h i -> p (h i)"))
-        warm = held.tile([P, 1], F32, name="warm")
-        nc.scalar.activation(warm[:], log_row[:, 0:1], ACT.Exp)
         for t in range(EARLY, PACK):
             nc.vector.tensor_tensor(part1[:, t, :], key_planes[t][:].indirect(list1[:]), share[:, 0, :], ALU.mult)
             nc.vector.tensor_tensor(part2[:, t, :], key_planes[t][:].indirect(list2[:]), share[:, 1, :], ALU.mult)
@@ -177,10 +174,7 @@ def tile_attend_bmassmerge_kernel(tc, query, keys, mass, target, qs, qrows, old,
         for r in range(PACK):
             nc.scalar.activation(scaled_target[:, r, :], target_sb[:, r, :], ACT.Copy, scale=qs_sb[:, r : r + 1])
 
-        qrows_codes = [
-            held.tile([P, D // 2], U32, tag=tag, name=f"qrows_codes{h}", align_bytes=64)
-            for h, tag in enumerate(("km_g", "qrows_codes1"))
-        ]
+        qrows_codes = [held.tile([P, D // 2], U32, tag="km_g", name="qrows_codes0", align_bytes=64)]
         qrows_scales = [held.tile([P, D // 2], U8, name=f"qrows_scales{h}", align_bytes=64) for h in range(2)]
 
         def weave_qrows(h, grouped):
@@ -213,12 +207,13 @@ def tile_attend_bmassmerge_kernel(tc, query, keys, mass, target, qs, qrows, old,
                     weighted[:, r, :], p[:, r, :], inv_sum[:, r : r + 1], qs_sb[:, r : r + 1], ALU.mult, ALU.mult
                 )
 
-        ds_g = held.tile([P, I * PACK], BF16, name="ds_g", align_bytes=64)
+        ds_g = held.tile([P, I * PACK], BF16, tag="ds_g", name="ds_g", align_bytes=64)
         ds_codes = held.tile([P, I], U32, name="ds_codes", align_bytes=64)
         ds_scales = held.tile([P, I], U8, name="ds_scales", align_bytes=64)
         for h in range(2):
             nc.vector.tensor_tensor(woven(ds_g, h), planes(weighted, h), planes(scaled_target, h), ALU.subtract)
             quantize_half(ds_codes, ds_scales, ds_g, h)
+        qrows_codes.append(held.tile([P, D // 2], U32, tag="ds_g", name="qrows_codes1", align_bytes=64))
         quantize_qrows(1, qrows_g1)
 
         def add_turned(j, src, first, last):
@@ -254,6 +249,9 @@ def tile_attend_bmassmerge_kernel(tc, query, keys, mass, target, qs, qrows, old,
         key_gradient(early_banks[0], [(0, slice(0, HALF))])
         key_gradient(early_banks[1], [(0, slice(HALF, I)), (1, slice(0, I))])
         key_gradient(early_banks[0], [(2, slice(0, I)), (3, slice(0, I))])
+
+        windows[1].append(held.tile([P, T], F32, tag="scores", name="window1_1", align_bytes=64))
+        nc.gpsimd.memset(windows[1][1][:], 0.0)
 
         def scatter(j, l, window):
             nc.vector.tensor_tensor(window[:].indirect(lists[l][:]), gk[:, j * I : (j + 1) * I], share[:, l, :], ALU.mult)

from contextlib import ExitStack

import concourse.mybir as mybir
from concourse.masks import make_identity

D, T, I, Q = 512, 1024, 256, 512
FLOPS = 2 * D * Q * I * 2

F32 = mybir.dt.float32
BF16 = mybir.dt.bfloat16
U32 = mybir.dt.uint32
U16 = mybir.dt.uint16
U8 = mybir.dt.uint8
FP8X4 = mybir.dt.float8_e4m3fn_x4
ALU = mybir.AluOpType
ACT = mybir.ActivationFunctionType
AX = mybir.AxisListType

P = 128
PACK = 4
HALF = I // 2
EARLY = 2
BANK = 512


def tile_attend_bmassmerge_kernel(tc, query, keys, mass, target, qs, qrows, old, offs, offs2, out):
    nc = tc.nc
    with ExitStack() as ctx:
        held = ctx.enter_context(tc.tile_pool(name="held", bufs=1))
        ring = ctx.enter_context(tc.tile_pool(name="ring", bufs=3))
        psum = ctx.enter_context(tc.psum_pool(name="psum", bufs=1))
        banks = [[psum.tile([P, PACK, P], F32, name=f"bank{j}_{u}") for u in range(2)] for j in range(PACK)]
        early_banks = banks[PACK - 1]

        list1 = held.tile([P, I // 16], U16, name="list1")
        list2 = held.tile([P, I // 16], U16, name="list2")
        lists = (list1, list2)
        mass_sb = held.tile([P, T], F32, name="mass_sb")
        key_planes = [held.tile([P, T], F32, tag=f"key_plane{t}", name=f"key_plane{t}") for t in range(PACK)]
        query_sb = [held.tile([P, PACK, Q // 2], F32, name=f"query_sb{h}") for h in range(2)]
        qrows_sb = [held.tile([P, PACK, D // 2], F32, name=f"qrows_sb{h}") for h in range(2)]
        target_sb = held.tile([P, PACK, I], F32, name="target_sb")
        qs_sb = held.tile([P, PACK], F32, name="qs_sb")

        keys_v = keys.rearrange("(p t) n -> p t n", t=PACK)
        query_v = query.rearrange("(p j) q -> p j q", j=PACK)
        qrows_v = qrows.rearrange("(p j) d -> p j d", j=PACK)
        nc.sync.dma_start(mass_sb[:], mass)
        nc.sync.dma_start(list1[:], offs)
        nc.sync.dma_start(list2[:], offs2)
        for t in range(PACK):
            nc.sync.dma_start(key_planes[t][:], keys_v[:, t, :])
        for h in range(2):
            nc.sync.dma_start(query_sb[h][:], query_v[:, :, h * (Q // 2) : (h + 1) * (Q // 2)])
        nc.sync.dma_start(qs_sb[:], qs.rearrange("(p r) o -> p (r o)", r=PACK))
        nc.sync.dma_start(target_sb[:], target.rearrange("(p r) i -> p r i", r=PACK))
        for h in range(2):
            nc.sync.dma_start(qrows_sb[h][:], qrows_v[:, :, h * (D // 2) : (h + 1) * (D // 2)])

        ident = held.tile([P, P], F32, name="ident")
        make_identity(nc, ident[:])
        windows = [[held.tile([P, T], F32, name=f"window{l}_{b}") for b in range(2 - l)] for l in range(2)]
        nc.vector.memset(windows[0][0][:], 0.0)
        nc.vector.memset(windows[0][1][:], 0.0)
        nc.gpsimd.memset(windows[1][0][:], 0.0)

        def turn(dst, src, start=True, stop=True):
            nc.tensor.matmul(dst, lhsT=src, rhs=ident[:], is_transpose=True, start=start, stop=stop)

        m = held.tile([P, 2, I], F32, name="m")
        for l in range(2):
            nc.vector.tensor_copy(m[:, l, :], mass_sb[:].indirect(lists[l][:]))
        joint_t = early_banks[0]
        for h in range(2):
            for l in range(2):
                turn(joint_t[:, h, :], m[:, l, h * HALF : (h + 1) * HALF], start=(l == 0), stop=(l == 1))

        part1 = held.tile([P, PACK, I], F32, tag="part1", name="part1")
        part2 = held.tile([P, PACK, I], F32, tag="part2", name="part2")
        diff = held.tile([P, EARLY, I], F32, tag="diff", name="diff", align_bytes=64)

        def gather_early(t):
            nc.vector.tensor_copy(part2[:, t, :], key_planes[t][:].indirect(list2[:]))
            nc.vector.tensor_tensor(diff[:, t, :], key_planes[t][:].indirect(list1[:]), part2[:, t, :], ALU.subtract)

        gather_early(0)
        inv_col = held.tile([P, 2], F32, name="inv_col")
        joint_col = part2[:, 1, 0:2]
        log_col = held.tile([P, 2], F32, name="log_col")
        nc.scalar.activation(log_col[:], joint_t[:, 0:2, 0], ACT.Ln)
        nc.scalar.copy(joint_col, joint_t[:, 0:2, 0])
        nc.vector.reciprocal(inv_col[:], joint_col)
        inv_row = early_banks[1][:, 0:2, :].rearrange("p h i -> p (h i)")
        for h in range(2):
            turn(inv_row[:, h * HALF : (h + 1) * HALF], inv_col[:, h : h + 1].to_broadcast([P, P]))
        gather_early(1)
        share = held.tile([P, 2, I], F32, name="share")
        nc.vector.tensor_tensor(share[:], m[:], inv_row.unsqueeze(1).to_broadcast([P, 2, I]), ALU.mult)
        log_row = held.tile([P, I], F32, name="log_row")
        for h in range(2):
            turn(joint_t[:, 2 + h, :], log_col[:, h : h + 1].to_broadcast([P, P]))
        nc.scalar.copy(log_row[:], joint_t[:, 2:4, :].rearrange("p h i -> p (h i)"))
        for t in range(EARLY, PACK):
            nc.vector.tensor_tensor(part1[:, t, :], key_planes[t][:].indirect(list1[:]), share[:, 0, :], ALU.mult)
            nc.vector.tensor_tensor(part2[:, t, :], key_planes[t][:].indirect(list2[:]), share[:, 1, :], ALU.mult)
        nc.vector.tensor_tensor(
            part1[:, 0:EARLY, :], diff[:], share[:, 0, :].unsqueeze(1).to_broadcast([P, EARLY, I]), ALU.mult
        )

        query_g = held.tile([P, PACK, P, PACK], BF16, name="query_g", align_bytes=64)
        for h in range(2):
            nc.scalar.copy(
                query_g[:, :, h * 64 : (h + 1) * 64, :].rearrange("p r s j -> p s j r"),
                query_sb[h][:].rearrange("p j (s r) -> p s j r", r=PACK),
            )
        query_codes = held.tile([P, Q], U32, tag="diff", name="query_codes", align_bytes=64)
        query_scales = held.tile([P, Q], U8, name="query_scales", align_bytes=64)

        km_g = held.tile([P, I * PACK], BF16, tag="km_g", name="km_g", align_bytes=64)
        km_codes = held.tile([P, I], U32, name="km_codes", align_bytes=64)
        km_scales = held.tile([P, I], U8, name="km_scales", align_bytes=64)

        def woven(tile, h):
            return tile[:, h * HALF * PACK : (h + 1) * HALF * PACK].rearrange("p (c i t) -> p c t i", i=4, t=PACK)

        def planes(tile, h):
            return tile[:, :, h * HALF : (h + 1) * HALF].rearrange("p t (c i) -> p c t i", i=4)

        def quantize_half(codes, scales, grouped, h):
            cols = slice(h * HALF, (h + 1) * HALF)
            nc.vector.quantize_mx(
                out=codes[:, cols].bitcast(FP8X4),
                scales=scales[:, cols],
                in_=grouped[:, h * HALF * PACK : (h + 1) * HALF * PACK],
            )

        nc.vector.tensor_tensor(
            km_g[:].rearrange("p (c i t) -> p c t i", i=4, t=PACK),
            part1[:].rearrange("p t (c i) -> p c t i", i=4),
            part2[:].rearrange("p t (c i) -> p c t i", i=4),
            ALU.add,
        )
        nc.vector.quantize_mx(
            out=query_codes[:].bitcast(FP8X4),
            scales=query_scales[:],
            in_=query_g[:].rearrange("p r s j -> p (r s j)"),
        )
        nc.vector.quantize_mx(out=km_codes[:].bitcast(FP8X4), scales=km_scales[:], in_=km_g[:])

        old_sb = []
        for j, freed in enumerate(("key_plane3", "part1", "part2", "key_plane2")):
            old_sb.append(held.tile([P, T], F32, tag=freed, name=f"old_sb{j}"))
            nc.sync.dma_start(old_sb[j][:], old[j * P : (j + 1) * P, :])

        s = held.tile([P, PACK, I], F32, tag="scores", name="s", align_bytes=64)
        neg_max = held.tile([P, PACK], F32, name="neg_max")
        pairs = [slice(0, 2), slice(2, 4)]
        for u, pair in enumerate(pairs):
            a = early_banks[u][:].rearrange("p (r h) i -> p r (h i)", r=2)
            for r in range(pair.start, pair.stop):
                nc.tensor.matmul_mx(
                    out=a[:, r - pair.start, :],
                    lhsT=query_codes[:, r * P : (r + 1) * P].bitcast(FP8X4),
                    lhsT_scale=query_scales[:, r * P : (r + 1) * P],
                    rhs=km_codes[:].bitcast(FP8X4),
                    rhs_scale=km_scales[:],
                    start=True,
                    stop=True,
                )
            nc.vector.tensor_tensor(s[:, pair, :], a, log_row[:].unsqueeze(1).to_broadcast([P, 2, I]), ALU.add)
            nc.vector.tensor_reduce(neg_max[:, pair], s[:, pair, :], AX.X, ALU.max, negate=True)

        scaled_target = held.tile([P, PACK, I], F32, name="scaled_target")
        for r in range(PACK):
            nc.scalar.activation(scaled_target[:, r, :], target_sb[:, r, :], ACT.Copy, scale=qs_sb[:, r : r + 1])

        qrows_codes = [held.tile([P, D // 2], U32, tag="km_g", name="qrows_codes0", align_bytes=64)]
        qrows_scales = [held.tile([P, D // 2], U8, name=f"qrows_scales{h}", align_bytes=64) for h in range(2)]

        def weave_qrows(h, grouped):
            nc.scalar.copy(
                grouped[:].rearrange("p (c i j) -> p c j i", i=4, j=PACK),
                qrows_sb[h][:].rearrange("p j (c i) -> p c j i", i=4),
            )

        def quantize_qrows(h, grouped):
            nc.vector.quantize_mx(out=qrows_codes[h][:].bitcast(FP8X4), scales=qrows_scales[h][:], in_=grouped[:])

        qrows_g0 = held.tile([P, D // 2 * PACK], BF16, name="qrows_g0", align_bytes=64)
        weave_qrows(0, qrows_g0)
        quantize_qrows(0, qrows_g0)

        row_sum = held.tile([P, PACK], F32, name="row_sum")
        inv_sum = held.tile([P, PACK], F32, name="inv_sum")
        p = held.tile([P, PACK, I], F32, name="p")
        weighted = held.tile([P, PACK, I], F32, name="weighted")
        for r in range(PACK):
            nc.scalar.activation(
                p[:, r, :], s[:, r, :], ACT.Exp, bias=neg_max[:, r : r + 1], accum_out=row_sum[:, r : r + 1]
            )
        qrows_g1 = held.tile([P, D // 2 * PACK], BF16, tag="scores", name="qrows_g1", align_bytes=64)
        weave_qrows(1, qrows_g1)
        for pair in pairs:
            nc.vector.reciprocal(inv_sum[:, pair], row_sum[:, pair])
            for r in range(pair.start, pair.stop):
                nc.vector.tensor_scalar(
                    weighted[:, r, :], p[:, r, :], inv_sum[:, r : r + 1], qs_sb[:, r : r + 1], ALU.mult, ALU.mult
                )

        ds_g = held.tile([P, I * PACK], BF16, tag="ds_g", name="ds_g", align_bytes=64)
        ds_codes = held.tile([P, I], U32, name="ds_codes", align_bytes=64)
        ds_scales = held.tile([P, I], U8, name="ds_scales", align_bytes=64)
        for h in range(2):
            nc.vector.tensor_tensor(woven(ds_g, h), planes(weighted, h), planes(scaled_target, h), ALU.subtract)
            quantize_half(ds_codes, ds_scales, ds_g, h)
        qrows_codes.append(held.tile([P, D // 2], U32, tag="ds_g", name="qrows_codes1", align_bytes=64))
        quantize_qrows(1, qrows_g1)

        def add_turned(j, src, first, last):
            for u in range(2):
                for b in range(PACK):
                    c0 = u * BANK + b * P
                    turn(banks[j][u][:, b, :], src[:, c0 : c0 + P], start=(first and b == 0), stop=(last and b == PACK - 1))

        for j in range(3):
            add_turned(j, old_sb[j], True, False)

        gk = held.tile([P, PACK * I], F32, name="gk")

        def key_gradient(bank, pieces):
            flat = bank[:].rearrange("p b i -> p (b i)")
            first = pieces[0][0] * I + pieces[0][1].start
            for j, cols in pieces:
                nc.tensor.matmul_mx(
                    out=flat[:, j * I + cols.start - first : j * I + cols.stop - first],
                    lhsT=qrows_codes[j // 2][:, j % 2 * P : (j % 2 + 1) * P].bitcast(FP8X4),
                    lhsT_scale=qrows_scales[j // 2][:, j % 2 * P : (j % 2 + 1) * P],
                    rhs=ds_codes[:, cols].bitcast(FP8X4),
                    rhs_scale=ds_scales[:, cols],
                    start=True,
                    stop=True,
                )
            for j, cols in pieces:
                nc.scalar.copy(
                    gk[:, j * I + cols.start : j * I + cols.stop],
                    flat[:, j * I + cols.start - first : j * I + cols.stop - first],
                )

        key_gradient(early_banks[0], [(0, slice(0, HALF))])
        key_gradient(early_banks[1], [(0, slice(HALF, I)), (1, slice(0, I))])
        key_gradient(early_banks[0], [(2, slice(0, I)), (3, slice(0, I))])

        windows[1].append(held.tile([P, T], F32, tag="scores", name="window1_1", align_bytes=64))
        nc.gpsimd.memset(windows[1][1][:], 0.0)

        def scatter(j, l, window):
            nc.vector.tensor_tensor(window[:].indirect(lists[l][:]), gk[:, j * I : (j + 1) * I], share[:, l, :], ALU.mult)

        def turn_back(j):
            for u in range(2):
                staged = ring.tile([P, PACK, P], F32, tag="staged", name="staged")
                nc.scalar.copy(staged[:], banks[j][u][:])
                for b in range(PACK):
                    turn(banks[j][u][:, b, :], staged[:, b, :])

        add_turned(3, old_sb[3], True, False)
        results = [held.tile([P, T], F32, name=f"result{j}") for j in range(PACK)]
        for h in range(2):
            cols = slice(h * HALF, (h + 1) * HALF)
            nc.vector.tensor_tensor(
                windows[0][0][:].indirect(list1[:, h * 8 : (h + 1) * 8]), gk[:, cols], share[:, 0, cols], ALU.mult
            )
        add_turned(0, windows[0][0], False, True)
        turn_back(0)
        for j, order in ((1, (0, 1)), (2, (1, 0))):
            for l in order:
                window = windows[l][(j + l) % 2]
                scatter(j, l, window)
                add_turned(j, window, False, l == order[1])
            turn_back(j)
            for u in range(2):
                nc.scalar.copy(results[j][:, u * BANK : (u + 1) * BANK], banks[j][u][:].rearrange("p b t -> p (b t)"))
            nc.scalar.dma_start(out[j * P : (j + 1) * P, :], results[j][:])
        scatter(3, 0, windows[0][1])
        add_turned(3, windows[0][1], False, True)
        turn_back(3)
        for j in (0, 3):
            window = windows[1][j % 2]
            scatter(j, 1, window)
            for u in range(2):
                cols = slice(u * BANK, (u + 1) * BANK)
                nc.vector.tensor_tensor(
                    results[j][:, cols], banks[j][u][:].rearrange("p b t -> p (b t)"), window[:, cols], ALU.add
                )
                nc.sync.dma_start(out[j * P : (j + 1) * P, cols], results[j][:, cols])
